import numpy as np
import ml_dtypes


def mxq(x, axis, fmt="e4m3"):
    dtype, down = {"e4m3": (ml_dtypes.float8_e4m3fn, 7), "e5m2": (ml_dtypes.float8_e5m2, 14)}[fmt]
    v = np.moveaxis(np.asarray(x, np.float32).astype(ml_dtypes.bfloat16).astype(np.float64), axis, -1)
    blocks = v.reshape(v.shape[:-1] + (-1, 32))
    amax = np.abs(blocks).max(-1, keepdims=True)
    byte = np.maximum(np.where(amax > 0, np.frexp(amax)[1] - 1 + 127, 0) - down, 1)
    scale = np.exp2(byte - 127.0)
    codes = (blocks / scale).astype(np.float32).astype(dtype).astype(np.float64)
    return np.moveaxis((codes * scale).reshape(v.shape), -1, axis)


WIDE = False


def mx_kscale(k):
    if not WIDE:
        return np.ones(k)
    levels = np.array([10, -10, 5, -5, 0])
    if k % 512:
        return np.exp2(np.random.permutation(np.resize(levels, k // 32))).repeat(32)
    a = np.empty((k // 512, 16))
    for p in range(k // 512):
        a[p, :8] = np.random.permutation(np.resize(levels, 8))
        for g in range(8):
            far = levels[np.abs(levels - a[p, g]) >= 10]
            a[p, g + 8] = far[np.random.randint(len(far))]
    return np.exp2(a.ravel()).repeat(32)


BF16 = ml_dtypes.bfloat16


def bf(x):
    return np.asarray(x, np.float32).astype(BF16)


def f64(x):
    return np.asarray(x).astype(np.float64)


E2M1 = np.array([0.0, 0.5, 1.0, 1.5, 2.0, 3.0, 4.0, 6.0, -0.0, -0.5, -1.0, -1.5, -2.0, -3.0, -4.0, -6.0])


def pack_weight(w, fmt):
    k, n = w.shape
    w = f64(bf(w)).reshape(k // 32, 32, n)
    amax = np.abs(w).max(1)
    if fmt == "e4m3":
        byte = np.frexp(amax)[1] - 1 + 127 - 7
    else:
        mant, ex = np.frexp(amax / 6.0)
        byte = np.where(mant > 0.5, ex, ex - 1) + 127
    byte = np.clip(np.where(amax > 0, byte, 1), 1, 254)
    scaled = (w * np.exp2(127.0 - byte)[:, None, :]).reshape(k, n).astype(np.float32)
    by_word = np.ascontiguousarray(scaled.reshape(k // 512, 128, 4, n).transpose(0, 1, 3, 2))
    if fmt == "e4m3":
        words = by_word.astype(ml_dtypes.float8_e4m3fn).view(np.uint8)
    else:
        c = by_word.astype(ml_dtypes.float4_e2m1fn).view(np.uint8) & 0xF
        words = c[..., 0::2] | (c[..., 1::2] << 4)
    return np.ascontiguousarray(words), np.ascontiguousarray(byte.astype(np.uint8).reshape(k // 512, 16, n))


def unpack_weight(words, scales, fmt):
    g, p, n, _ = words.shape
    if fmt == "e4m3":
        vals = np.ascontiguousarray(words).view(ml_dtypes.float8_e4m3fn).astype(np.float64)
    else:
        nib = np.empty((g, p, n, 4), np.uint8)
        nib[..., 0::2] = words & 0xF
        nib[..., 1::2] = words >> 4
        vals = E2M1[nib]
    vals = vals * np.repeat(np.exp2(scales.astype(np.float64) - 127.0), 8, axis=1)[..., None]
    return vals.transpose(0, 1, 3, 2).reshape(g * 512, n)
def pack4(w):
    words, scales = pack_weight(w, "e2m1")
    return words.reshape(words.shape[0], 128, -1), scales


def unpack4(words, scales):
    return unpack_weight(words.reshape(words.shape[0], 128, -1, 2), scales, "e2m1")


B, N, P, R = 1024, 1024, 2048, 512


def setup_inputs():
    s = mx_kscale(N)
    r = mx_kscale(R)
    t = mx_kscale(N)
    hard_inv = np.random.standard_normal((N, N)) / np.sqrt(N) + 1.0 / N
    h_words, h_scales = pack4(hard_inv / s[:, None])
    return {"chi": bf((0.5 + np.random.standard_normal((B, N))) * s),
            "h_words": h_words,
            "h_scales": h_scales,
            "screen": bf((1.0 + 0.1 * np.random.standard_normal(N)) * t),
            "probe": bf(np.random.standard_normal((P, R)) * r),
            "atom": bf(np.random.standard_normal((R, N)) / np.sqrt(R) / N ** 0.25 / r[:, None] / t)}


def reference(chi, h_words, h_scales, screen, probe, atom):
    a = mxq(f64(chi), 1, "e4m3") @ unpack4(h_words, h_scales)
    charge = (a.mean(axis=1, keepdims=True) - a) * f64(screen)
    kernel = mxq(f64(probe), 1, "e4m3") @ mxq(f64(atom), 0, "e4m3")
    return mxq(charge, 1, "e4m3") @ mxq(kernel, 1, "e4m3").T

@@ -1,0 +1,242 @@
+from contextlib import ExitStack
+
+import concourse.mybir as mybir
+from concourse.masks import make_identity
+
+B, N, P, R = 1024, 1024, 2048, 512
+FLOPS = 2 * (B * N * N + P * R * N + B * N * P)
+
+F32 = mybir.dt.float32
+BF16 = mybir.dt.bfloat16
+U32 = mybir.dt.uint32
+I32 = mybir.dt.int32
+U8 = mybir.dt.uint8
+FP8X4 = mybir.dt.float8_e4m3fn_x4
+FP4X4 = mybir.dt.float4_e2m1fn_x4
+ALU = mybir.AluOpType
+ACT = mybir.ActivationFunctionType
+
+ORDER = [("w", 3, "S"), ("tc", 0, "S"), ("la", 0, "V"), ("la", 1, "V"), ("tc", 1, "S"), ("sc", 0, "S"), ("sc", 1, "S"), ("qc", 0, "S"), ("qa", 0, "S"), ("a", 0, "S"), ("qc", 1, "S"), ("a", 1, "S"), ("tp", 0, "S"), ("la", 2, "V"), ("la", 3, "V"), ("qp", 0, "S"), ("qa", 1, "S"), ("tc", 2, "S"), ("tp", 1, "S"), ("m", 0, "S"), ("a", 2, "S"), ("c", 0, "S"), ("a", 3, "S"), ("qc", 2, "S"), ("qp", 1, "S"), ("k", 0, "V"), ("k", 1, "S"), ("k", 2, "V"), ("k", 3, "S"), ("tq", 0, "S"), ("tc", 3, "S"), ("tp", 2, "S"), ("m", 1, "S"), ("a", 4, "S"), ("c", 1, "S"), ("a", 5, "S"), ("qq", 0, "S"), ("qc", 3, "S"), ("qp", 2, "S"), ("k", 4, "V"), ("k", 5, "S"), ("k", 6, "V"), ("k", 7, "S"), ("tq", 1, "S"), ("tc", 4, "S"), ("tp", 3, "S"), ("qk", 0, "S"), ("qk", 1, "S"), ("m", 2, "S"), ("a", 6, "S"), ("c", 2, "S"), ("a", 7, "S"), ("qq", 1, "S"), ("qc", 4, "S"), ("qp", 3, "S"), ("k", 8, "V"), ("o", 0, "S"), ("k", 9, "V"), ("k", 10, "S"), ("k", 11, "V"), ("tq", 2, "S"), ("tc", 5, "S"), ("tp", 4, "S"), ("m", 3, "S"), ("a", 8, "S"), ("c", 3, "S"), ("a", 9, "S"), ("qq", 2, "S"), ("qc", 5, "S"), ("qp", 4, "S"), ("k", 12, "S"), ("o", 4, "V"), ("k", 13, "S"), ("k", 14, "V"), ("o", 8, "S"), ("k", 15, "V"), ("tq", 3, "S"), ("tc", 6, "S"), ("tp", 5, "S"), ("qk", 2, "S"), ("qk", 3, "S"), ("m", 4, "S"), ("a", 10, "S"), ("c", 4, "S"), ("a", 11, "S"), ("qq", 3, "S"), ("qc", 6, "S"), ("qp", 5, "S"), ("k", 16, "S"), ("o", 1, "V"), ("k", 17, "S"), ("k", 18, "V"), ("o", 5, "S"), ("k", 19, "V"), ("o", 9, "S"), ("tq", 4, "S"), ("tc", 7, "S"), ("tp", 6, "S"), ("m", 5, "S"), ("a", 12, "S"), ("c", 5, "S"), ("a", 13, "S"), ("qq", 4, "S"), ("qc", 7, "S"), ("qp", 6, "S"), ("k", 20, "V"), ("o", 12, "S"), ("k", 21, "V"), ("k", 22, "S"), ("o", 13, "V"), ("k", 23, "S"), ("o", 16, "V"), ("tq", 5, "S"), ("tp", 7, "S"), ("qk", 4, "S"), ("qk", 5, "S"), ("m", 6, "S"), ("a", 14, "S"), ("c", 6, "S"), ("a", 15, "S"), ("qq", 5, "S"), ("qp", 7, "S"), ("k", 24, "S"), ("o", 17, "V"), ("k", 25, "S"), ("o", 2, "V"), ("k", 26, "S"), ("o", 6, "V"), ("k", 27, "S"), ("o", 10, "V"), ("tq", 6, "S"), ("m", 7, "S"), ("c", 7, "S"), ("qq", 6, "S"), ("k", 28, "S"), ("o", 14, "V"), ("k", 29, "S"), ("o", 18, "V"), ("k", 30, "S"), ("o", 20, "V"), ("k", 31, "S"), ("o", 21, "V"), ("tq", 7, "S"), ("qk", 6, "S"), ("qk", 7, "S"), ("qq", 7, "S"), ("o", 22, "S"), ("o", 24, "V"), ("o", 25, "S"), ("o", 26, "V"), ("o", 3, "S"), ("o", 7, "V"), ("o", 11, "S"), ("o", 15, "V"), ("o", 19, "S"), ("o", 23, "V"), ("o", 27, "S"), ("o", 28, "V"), ("o", 29, "S"), ("o", 30, "V"), ("o", 31, "S")]
+LOADS = [("chi", 0), ("atom", 0), ("s", 0), ("hs", 0), ("hs", 1), ("hs", 2), ("hs", 3), ("chi", 1), ("h", 0), ("probe", 0), ("atom", 1), ("chi", 2), ("probe", 1), ("probe", 2), ("chi", 3), ("probe", 3), ("chi", 4), ("probe", 4), ("chi", 5), ("probe", 5), ("chi", 6), ("probe", 6), ("chi", 7), ("probe", 7)]
+
+
+def tile_projected_response_charge_potentials_s11_kernel(tc, chi, h_words, h_scales, screen, probe, atom, out):
+    nc = tc.nc
+    with ExitStack() as ctx:
+        keep = ctx.enter_context(tc.tile_pool(name="keep", bufs=1))
+        stage = ctx.enter_context(tc.tile_pool(name="stage", bufs=3))
+        psum = ctx.enter_context(tc.psum_pool(name="psum", bufs=8))
+        ctx.enter_context(tc.manual_schedule())
+
+        def kept(name, shape, dtype):
+            return keep.tile(shape, dtype, name=name, align_bytes=64)
+
+        def staged(name, shape, dtype, bufs):
+            return stage.tile(shape, dtype, name=name, bufs=bufs, align_bytes=64)
+
+        def bank():
+            return psum.tile([128, 512], F32, name="bank")
+
+        def copy_on(engine, dst, src):
+            if engine == "S":
+                nc.scalar.copy(out=dst, in_=src)
+            else:
+                nc.vector.tensor_copy(out=dst, in_=src)
+
+        def quantise(name, src):
+            width = src.shape[1] // 4
+            codes = kept(name + "_codes", [128, width], U32)
+            scales = kept(name + "_scales", [128, width], U8)
+            nc.vector.quantize_mx(out=codes[:].bitcast(FP8X4), scales=scales[:], in_=src)
+            return codes, scales
+
+        ident = kept("ident", [128, 128], F32)
+        make_identity(nc, ident[:])
+        screen_row = kept("screen_row", [128, N], BF16)
+        nc.vector.memset(screen_row[:].bitcast(I32), 0)
+        ones = kept("ones", [128, 512], BF16)
+        nc.vector.memset(ones[:], 1.0)
+        h_plane = kept("h_plane", [128, 2 * N], U8)
+        nc.vector.memset(h_plane[:].bitcast(I32), 0)
+        warm = kept("warm", [128, 1], F32)
+        nc.scalar.activation(out=warm[:], in_=ones[:, 0:1], func=ACT.Copy)
+
+        chi_raw, probe_raw, atom_raw = {}, {}, {}
+        h_codes = kept("h_codes", [128, 2 * 2 * N], U8)
+        for kind, i in LOADS:
+            if kind == "chi":
+                chi_raw[i] = kept("chi_raw%d" % i, [128, N], BF16)
+                nc.sync.dma_start(out=chi_raw[i][:], in_=chi[128 * i : 128 * (i + 1), :])
+            elif kind == "probe":
+                probe_raw[i] = kept("probe_raw%d" % i, [128, 2 * R], BF16)
+                nc.sync.dma_start(out=probe_raw[i][:], in_=probe[256 * i : 256 * (i + 1), :].rearrange("(p a) k -> p (a k)", a=2))
+            elif kind == "atom":
+                atom_raw[i] = kept("atom_raw%d" % i, [128, 4, 512], BF16)
+                nc.sync.dma_start(out=atom_raw[i][:], in_=atom[:, 512 * i : 512 * (i + 1)].rearrange("(p j) n -> p j n", j=4))
+            elif kind == "h":
+                nc.sync.dma_start(out=h_codes[:].bitcast(I32).rearrange("p (g n) -> p g n", g=2), in_=h_words.bitcast(I32).rearrange("g p n -> p g n"))
+            elif kind == "hs":
+                nc.sync.dma_start(
+                    out=h_plane[i:128:32, :].bitcast(I32).rearrange("p (g n) -> p g n", g=2),
+                    in_=h_scales.bitcast(I32).rearrange("g (q r) n -> r q g n", r=4)[i],
+                )
+            else:
+                nc.sync.dma_start(out=screen_row[0:1, :], in_=screen.rearrange("(o n) -> o n", o=1))
+
+        def sorted_view(ap):
+            return ap.rearrange("p (w e r) -> p w r e", e=2, r=8)
+
+        def dense_view(ap):
+            return ap.rearrange("p (w r e) -> p w r e", r=8, e=2)
+
+        screen_all = kept("screen_all", [128, N], F32)
+        chi_in, chi_q, neg_a, sums, mean, charge, charge_in, charge_q = {}, {}, {}, {}, {}, {}, {}, {}
+        probe_in, probe_q, atom_in, atom_q, kern_in, kern_q = {}, {}, {}, {}, {}, {}
+
+        def spread_screen(g, engine):
+            acc = bank()
+            nc.tensor.matmul(out=acc[:], lhsT=ones[:, 0:128], rhs=screen_row[:, 512 * g : 512 * (g + 1)], start=True, stop=True)
+            copy_on(engine, dense_view(screen_all[:, 512 * g : 512 * (g + 1)]), sorted_view(acc[:]))
+
+        def warm_up(n, engine):
+            acc = bank()
+            for w in range(n):
+                nc.tensor.matmul(out=acc[:], lhsT=ones[:, 0:128], rhs=ones[:], start=True, stop=True)
+
+        def turn(words_of, dst, engine, pattern):
+            acc = bank()
+            for c in range(4):
+                nc.tensor.transpose(acc[:, 128 * c : 128 * (c + 1)], words_of(c // 2, c % 2), ident[:])
+            copy_on(engine, dst[:].bitcast(F32).rearrange(pattern[0], **pattern[2]), acc[:].rearrange(pattern[1], **pattern[2]))
+
+        by_group = ("p (g b u) -> p g b u", "p (g u b) -> p g b u", dict(g=2, u=2))
+        by_row_pair = ("p (m a u) -> p m a u", "p (a u m) -> p m a u", dict(a=2, u=2))
+
+        def turn_chi(i, engine):
+            words = chi_raw[i][:].bitcast(F32)
+            chi_in[i] = staged("chi_in", [128, N], BF16, 3)
+            turn(lambda g, u: words[:, 256 * g + u : 256 * (g + 1) : 2], chi_in[i], engine, by_group)
+
+        def turn_probe(i, engine):
+            words = probe_raw[i][:].bitcast(F32)
+            probe_in[i] = staged("probe_in", [128, 2 * R], BF16, 3)
+            turn(lambda a, u: words[:, 256 * a + u : 256 * (a + 1) : 2], probe_in[i], engine, by_row_pair)
+
+        def turn_charge(i, engine):
+            words = charge[i][:].bitcast(F32)
+            charge_in[i] = staged("charge_in", [128, N], BF16, 3)
+            turn(lambda g, u: words[:, 256 * u + 128 * g : 256 * u + 128 * (g + 1)], charge_in[i], engine, by_group)
+
+        def quant_chi(i, engine):
+            chi_q[i] = quantise("chi%d" % i, chi_in[i][:])
+
+        def quant_probe(i, engine):
+            probe_q[i] = quantise("probe%d" % i, probe_in[i][:])
+
+        def quant_charge(i, engine):
+            charge_q[i] = quantise("charge%d" % i, charge_in[i][:])
+
+        def lay_atom(gu, engine):
+            g, u = divmod(gu, 2)
+            if g not in atom_in:
+                atom_in[g] = kept("atom_in%d" % g, [128, 2048], BF16)
+            copy_on(
+                engine,
+                atom_in[g][:].rearrange("p (t q r j) -> p t q r j", t=4, r=8, j=4)[:, 2 * u : 2 * u + 2],
+                atom_raw[g][:].rearrange("p j (q t r) -> p t q r j", t=4, r=8)[:, 2 * u : 2 * u + 2],
+            )
+
+        def quant_atom(g, engine):
+            atom_q[g] = quantise("atom%d" % g, atom_in[g][:])
+
+        def response(ih, engine):
+            i, h = divmod(ih, 2)
+            if h == 0:
+                neg_a[i] = staged("neg_a", [128, N], F32, 3)
+                sums[i] = staged("sums", [128, 2], F32, 3)
+            codes, scales = chi_q[i]
+            acc = bank()
+            for g in range(2):
+                c0 = N * g + 512 * h
+                nc.tensor.matmul_mx(
+                    out=acc[:],
+                    lhsT=codes[:, 128 * g : 128 * (g + 1)].bitcast(FP8X4),
+                    lhsT_scale=scales[:, 128 * g : 128 * (g + 1)],
+                    rhs=h_codes[:, 2 * c0 : 2 * (c0 + 512)].bitcast(FP4X4),
+                    rhs_scale=h_plane[:, c0 : c0 + 512],
+                    start=(g == 0),
+                    stop=(g == 1),
+                )
+            dst = dense_view(neg_a[i][:, 512 * h : 512 * (h + 1)])
+            if engine == "S":
+                nc.scalar.activation(out=dst, in_=sorted_view(acc[:]), func=ACT.Copy, scale=-1.0, accum_out=sums[i][:, h : h + 1])
+            else:
+                nc.vector.tensor_scalar(out=dst, in0=sorted_view(acc[:]), scalar1=-1.0, scalar2=None, op0=ALU.mult, op1=ALU.add, accum_out=sums[i][:, h : h + 1])
+
+        def take_mean(i, engine):
+            mean[i] = staged("mean", [128, 1], F32, 3)
+            nc.vector.tensor_scalar(out=mean[i][:], in0=sums[i][:, 0:1], scalar1=sums[i][:, 1:2], scalar2=1.0 / N, op0=ALU.add, op1=ALU.mult)
+
+        def make_charge(i, engine):
+            charge[i] = staged("charge", [128, N], BF16, 3)
+            for u in range(2):
+                nc.vector.scalar_tensor_tensor(
+                    out=charge[i][:, 512 * u : 512 * (u + 1)].rearrange("p (w c) -> p w c", c=16),
+                    in0=neg_a[i][:].rearrange("p (w u c) -> p u w c", u=2, c=16)[:, u],
+                    scalar=mean[i][:],
+                    in1=screen_all[:].rearrange("p (w u c) -> p u w c", u=2, c=16)[:, u],
+                    op0=ALU.subtract,
+                    op1=ALU.mult,
+                )
+
+        def coulomb(jg, engine):
+            j, g = divmod(jg, 2)
+            key = (j // 4, g)
+            if j % 4 == 0:
+                kern_in[key] = staged("kern_in", [128, 2048], BF16, 4)
+            a_codes, a_scales = atom_q[g]
+            p_codes, p_scales = probe_q[j // 2]
+            cols = slice(128 * (j % 2), 128 * (j % 2 + 1))
+            acc = bank()
+            for t in range(4):
+                nc.tensor.matmul_mx(
+                    out=acc[:, 128 * t : 128 * (t + 1)],
+                    lhsT=a_codes[:, 128 * t : 128 * (t + 1)].bitcast(FP8X4),
+                    lhsT_scale=a_scales[:, 128 * t : 128 * (t + 1)],
+                    rhs=p_codes[:, cols].bitcast(FP8X4),
+                    rhs_scale=p_scales[:, cols],
+                    start=True,
+                    stop=True,
+                )
+            dst = kern_in[key][:, 512 * (j % 4) : 512 * (j % 4 + 1)]
+            copy_on(engine, dst.rearrange("p (m t) -> p m t", t=4), acc[:].rearrange("p (t m) -> p m t", t=4))
+
+        def quant_kern(cg, engine):
+            key = divmod(cg, 2)
+            kern_q[key] = quantise("kern%d" % cg, kern_in[key][:])
+
+        def potential(ic, engine):
+            i, c = divmod(ic, 4)
+            codes, scales = charge_q[i]
+            acc = bank()
+            for g in range(2):
+                k_codes, k_scales = kern_q[(c, g)]
+                nc.tensor.matmul_mx(
+                    out=acc[:],
+                    lhsT=codes[:, 128 * g : 128 * (g + 1)].bitcast(FP8X4),
+                    lhsT_scale=scales[:, 128 * g : 128 * (g + 1)],
+                    rhs=k_codes[:].bitcast(FP8X4),
+                    rhs_scale=k_scales[:],
+                    start=(g == 0),
+                    stop=(g == 1),
+                )
+            result = staged("result", [128, 512], F32, 10)
+            copy_on(engine, result[:], acc[:])
+            nc.sync.dma_start(out=out[128 * i : 128 * (i + 1), 512 * c : 512 * (c + 1)], in_=result[:])
+
+        steps = dict(
+            sc=spread_screen, w=warm_up, tc=turn_chi, tp=turn_probe, tq=turn_charge, qc=quant_chi, qp=quant_probe, qq=quant_charge,
+            la=lay_atom, qa=quant_atom, a=response, m=take_mean, c=make_charge, k=coulomb, qk=quant_kern, o=potential,
+        )
+        for kind, index, engine in ORDER:
+            steps[kind](index, engine)

@@ -16,8 +16,8 @@ FP4X4 = mybir.dt.float4_e2m1fn_x4
 ALU = mybir.AluOpType
 ACT = mybir.ActivationFunctionType
 
-ORDER = [("w", 3, "S"), ("tc", 0, "S"), ("la", 0, "V"), ("la", 1, "V"), ("tc", 1, "S"), ("sc", 0, "S"), ("sc", 1, "S"), ("qc", 0, "S"), ("qa", 0, "S"), ("a", 0, "S"), ("qc", 1, "S"), ("a", 1, "S"), ("tp", 0, "S"), ("la", 2, "V"), ("la", 3, "V"), ("qp", 0, "S"), ("qa", 1, "S"), ("tc", 2, "S"), ("tp", 1, "S"), ("m", 0, "S"), ("a", 2, "S"), ("c", 0, "S"), ("a", 3, "S"), ("qc", 2, "S"), ("qp", 1, "S"), ("k", 0, "V"), ("k", 1, "S"), ("k", 2, "V"), ("k", 3, "S"), ("tq", 0, "S"), ("tc", 3, "S"), ("tp", 2, "S"), ("m", 1, "S"), ("a", 4, "S"), ("c", 1, "S"), ("a", 5, "S"), ("qq", 0, "S"), ("qc", 3, "S"), ("qp", 2, "S"), ("k", 4, "V"), ("k", 5, "S"), ("k", 6, "V"), ("k", 7, "S"), ("tq", 1, "S"), ("tc", 4, "S"), ("tp", 3, "S"), ("qk", 0, "S"), ("qk", 1, "S"), ("m", 2, "S"), ("a", 6, "S"), ("c", 2, "S"), ("a", 7, "S"), ("qq", 1, "S"), ("qc", 4, "S"), ("qp", 3, "S"), ("k", 8, "V"), ("o", 0, "S"), ("k", 9, "V"), ("k", 10, "S"), ("k", 11, "V"), ("tq", 2, "S"), ("tc", 5, "S"), ("tp", 4, "S"), ("m", 3, "S"), ("a", 8, "S"), ("c", 3, "S"), ("a", 9, "S"), ("qq", 2, "S"), ("qc", 5, "S"), ("qp", 4, "S"), ("k", 12, "S"), ("o", 4, "V"), ("k", 13, "S"), ("k", 14, "V"), ("o", 8, "S"), ("k", 15, "V"), ("tq", 3, "S"), ("tc", 6, "S"), ("tp", 5, "S"), ("qk", 2, "S"), ("qk", 3, "S"), ("m", 4, "S"), ("a", 10, "S"), ("c", 4, "S"), ("a", 11, "S"), ("qq", 3, "S"), ("qc", 6, "S"), ("qp", 5, "S"), ("k", 16, "S"), ("o", 1, "V"), ("k", 17, "S"), ("k", 18, "V"), ("o", 5, "S"), ("k", 19, "V"), ("o", 9, "S"), ("tq", 4, "S"), ("tc", 7, "S"), ("tp", 6, "S"), ("m", 5, "S"), ("a", 12, "S"), ("c", 5, "S"), ("a", 13, "S"), ("qq", 4, "S"), ("qc", 7, "S"), ("qp", 6, "S"), ("k", 20, "V"), ("o", 12, "S"), ("k", 21, "V"), ("k", 22, "S"), ("o", 13, "V"), ("k", 23, "S"), ("o", 16, "V"), ("tq", 5, "S"), ("tp", 7, "S"), ("qk", 4, "S"), ("qk", 5, "S"), ("m", 6, "S"), ("a", 14, "S"), ("c", 6, "S"), ("a", 15, "S"), ("qq", 5, "S"), ("qp", 7, "S"), ("k", 24, "S"), ("o", 17, "V"), ("k", 25, "S"), ("o", 2, "V"), ("k", 26, "S"), ("o", 6, "V"), ("k", 27, "S"), ("o", 10, "V"), ("tq", 6, "S"), ("m", 7, "S"), ("c", 7, "S"), ("qq", 6, "S"), ("k", 28, "S"), ("o", 14, "V"), ("k", 29, "S"), ("o", 18, "V"), ("k", 30, "S"), ("o", 20, "V"), ("k", 31, "S"), ("o", 21, "V"), ("tq", 7, "S"), ("qk", 6, "S"), ("qk", 7, "S"), ("qq", 7, "S"), ("o", 22, "S"), ("o", 24, "V"), ("o", 25, "S"), ("o", 26, "V"), ("o", 3, "S"), ("o", 7, "V"), ("o", 11, "S"), ("o", 15, "V"), ("o", 19, "S"), ("o", 23, "V"), ("o", 27, "S"), ("o", 28, "V"), ("o", 29, "S"), ("o", 30, "V"), ("o", 31, "S")]
-LOADS = [("chi", 0), ("atom", 0), ("s", 0), ("hs", 0), ("hs", 1), ("hs", 2), ("hs", 3), ("chi", 1), ("h", 0), ("probe", 0), ("atom", 1), ("chi", 2), ("probe", 1), ("probe", 2), ("chi", 3), ("probe", 3), ("chi", 4), ("probe", 4), ("chi", 5), ("probe", 5), ("chi", 6), ("probe", 6), ("chi", 7), ("probe", 7)]
+ORDER = [("w", 4, "S"), ("tc", 0, "S"), ("la", 0, "V"), ("la", 1, "V"), ("tc", 1, "S"), ("sc", 0, "S"), ("sc", 1, "S"), ("qc", 0, "S"), ("qa", 0, "S"), ("a", 0, "S"), ("qc", 1, "S"), ("a", 1, "S"), ("tp", 0, "S"), ("la", 2, "V"), ("la", 3, "V"), ("qp", 0, "S"), ("qa", 1, "S"), ("m", 0, "S"), ("tc", 2, "S"), ("tp", 1, "S"), ("a", 2, "S"), ("c", 0, "S"), ("a", 3, "S"), ("qc", 2, "S"), ("qp", 1, "S"), ("k", 0, "S"), ("k", 1, "V"), ("m", 1, "S"), ("k", 2, "S"), ("k", 3, "V"), ("tq", 0, "S"), ("tc", 3, "S"), ("tp", 2, "S"), ("a", 4, "S"), ("c", 1, "S"), ("a", 5, "S"), ("qq", 0, "S"), ("qc", 3, "S"), ("qp", 2, "S"), ("xc", 4, "V"), ("xp", 3, "V"), ("k", 4, "S"), ("k", 5, "S"), ("m", 2, "S"), ("k", 6, "V"), ("k", 7, "S"), ("tq", 1, "S"), ("tc", 4, "S"), ("tp", 3, "S"), ("qk", 0, "S"), ("qk", 1, "S"), ("a", 6, "S"), ("c", 2, "S"), ("a", 7, "S"), ("qq", 1, "S"), ("qc", 4, "S"), ("qp", 3, "S"), ("xc", 5, "V"), ("xp", 4, "V"), ("k", 8, "V"), ("o", 0, "S"), ("m", 3, "S"), ("k", 9, "S"), ("k", 10, "V"), ("k", 11, "S"), ("tq", 2, "S"), ("tc", 5, "S"), ("tp", 4, "S"), ("a", 8, "S"), ("c", 3, "S"), ("a", 9, "S"), ("qq", 2, "S"), ("qc", 5, "S"), ("qp", 4, "S"), ("xc", 6, "V"), ("xp", 5, "V"), ("k", 12, "V"), ("o", 4, "S"), ("m", 4, "S"), ("k", 13, "S"), ("k", 14, "V"), ("o", 8, "S"), ("k", 15, "V"), ("tq", 3, "S"), ("tc", 6, "S"), ("tp", 5, "S"), ("qk", 2, "S"), ("qk", 3, "S"), ("a", 10, "S"), ("c", 4, "S"), ("a", 11, "S"), ("qq", 3, "S"), ("qc", 6, "S"), ("qp", 5, "S"), ("xc", 7, "V"), ("xp", 6, "V"), ("k", 16, "S"), ("o", 1, "S"), ("m", 5, "S"), ("k", 17, "V"), ("k", 18, "S"), ("o", 5, "V"), ("k", 19, "S"), ("o", 9, "S"), ("tq", 4, "S"), ("tc", 7, "S"), ("tp", 6, "S"), ("a", 12, "S"), ("c", 5, "S"), ("a", 13, "S"), ("qq", 4, "S"), ("qc", 7, "S"), ("qp", 6, "S"), ("xp", 7, "V"), ("k", 20, "V"), ("o", 12, "S"), ("m", 6, "S"), ("k", 21, "V"), ("k", 22, "S"), ("o", 13, "S"), ("k", 23, "V"), ("o", 16, "S"), ("tq", 5, "S"), ("tp", 7, "S"), ("qk", 4, "S"), ("qk", 5, "S"), ("a", 14, "S"), ("c", 6, "S"), ("a", 15, "S"), ("qq", 5, "S"), ("qp", 7, "S"), ("k", 24, "V"), ("o", 17, "S"), ("m", 7, "S"), ("k", 25, "S"), ("o", 2, "V"), ("k", 26, "S"), ("o", 6, "V"), ("k", 27, "S"), ("o", 10, "S"), ("tq", 6, "S"), ("c", 7, "S"), ("qq", 6, "S"), ("k", 28, "V"), ("o", 14, "S"), ("k", 29, "V"), ("o", 18, "S"), ("k", 30, "S"), ("o", 20, "V"), ("k", 31, "S"), ("o", 21, "V"), ("tq", 7, "S"), ("qk", 6, "S"), ("qk", 7, "S"), ("qq", 7, "S"), ("o", 22, "S"), ("o", 24, "S"), ("o", 25, "V"), ("o", 26, "S"), ("o", 3, "V"), ("o", 7, "S"), ("o", 11, "S"), ("o", 15, "V"), ("o", 19, "S"), ("o", 23, "V"), ("o", 27, "S"), ("o", 28, "S"), ("o", 29, "V"), ("o", 30, "S"), ("o", 31, "V")]
+LOADS = [("chi", 0), ("atom", 0), ("s", 0), ("hs", 0), ("hs", 1), ("hs", 2), ("hs", 3), ("chi", 1), ("h", 0), ("h", 1), ("probe", 0), ("atom", 1), ("chi", 2), ("probe", 1), ("probe", 2), ("chi", 3), ("probe", 3), ("chi", 4), ("probe", 4), ("chi", 5), ("probe", 5), ("chi", 6), ("probe", 6), ("chi", 7), ("probe", 7)]
 
 
 def tile_projected_response_charge_potentials_s11_kernel(tc, chi, h_words, h_scales, screen, probe, atom, out):
@@ -52,17 +52,17 @@ def tile_projected_response_charge_potentials_s11_kernel(tc, chi, h_words, h_sca
 
         ident = kept("ident", [128, 128], F32)
         make_identity(nc, ident[:])
-        screen_row = kept("screen_row", [128, N], BF16)
-        nc.vector.memset(screen_row[:].bitcast(I32), 0)
         ones = kept("ones", [128, 512], BF16)
         nc.vector.memset(ones[:], 1.0)
+        screen_row = kept("screen_row", [128, N], BF16)
+        nc.vector.memset(screen_row[:].bitcast(I32), 0)
         h_plane = kept("h_plane", [128, 2 * N], U8)
         nc.vector.memset(h_plane[:].bitcast(I32), 0)
         warm = kept("warm", [128, 1], F32)
         nc.scalar.activation(out=warm[:], in_=ones[:, 0:1], func=ACT.Copy)
 
         chi_raw, probe_raw, atom_raw = {}, {}, {}
-        h_codes = kept("h_codes", [128, 2 * 2 * N], U8)
+        h_codes = {}
         for kind, i in LOADS:
             if kind == "chi":
                 chi_raw[i] = kept("chi_raw%d" % i, [128, N], BF16)
@@ -74,7 +74,11 @@ def tile_projected_response_charge_potentials_s11_kernel(tc, chi, h_words, h_sca
                 atom_raw[i] = kept("atom_raw%d" % i, [128, 4, 512], BF16)
                 nc.sync.dma_start(out=atom_raw[i][:], in_=atom[:, 512 * i : 512 * (i + 1)].rearrange("(p j) n -> p j n", j=4))
             elif kind == "h":
-                nc.sync.dma_start(out=h_codes[:].bitcast(I32).rearrange("p (g n) -> p g n", g=2), in_=h_words.bitcast(I32).rearrange("g p n -> p g n"))
+                h_codes[i] = kept("h_codes%d" % i, [128, 2 * N], U8)
+                nc.sync.dma_start(
+                    out=h_codes[i][:].bitcast(I32).rearrange("p (g n) -> p g n", g=2),
+                    in_=h_words.bitcast(I32)[:, :, 256 * i : 256 * (i + 1)].rearrange("g p n -> p g n"),
+                )
             elif kind == "hs":
                 nc.sync.dma_start(
                     out=h_plane[i:128:32, :].bitcast(I32).rearrange("p (g n) -> p g n", g=2),
@@ -112,15 +116,34 @@ def tile_projected_response_charge_potentials_s11_kernel(tc, chi, h_words, h_sca
         by_group = ("p (g b u) -> p g b u", "p (g u b) -> p g b u", dict(g=2, u=2))
         by_row_pair = ("p (m a u) -> p m a u", "p (a u m) -> p m a u", dict(a=2, u=2))
 
+        split = {}
+
+        def split_words(name, raw, engine):
+            split[name] = staged("split", [128, 512], F32, 4)
+            copy_on(
+                engine,
+                split[name][:].rearrange("p (u c i) -> p c u i", u=2, i=4),
+                raw[:].bitcast(F32).rearrange("p (c i u) -> p c u i", u=2, i=4),
+            )
+
+        def split_chi(i, engine):
+            split_words(("chi", i), chi_raw[i], engine)
+
+        def split_probe(i, engine):
+            split_words(("probe", i), probe_raw[i], engine)
+
+        def words_of(name, raw):
+            if name in split:
+                return lambda g, u: split[name][:, 256 * u + 128 * g : 256 * u + 128 * (g + 1)]
+            return lambda g, u: raw[:].bitcast(F32)[:, 256 * g + u : 256 * (g + 1) : 2]
+
         def turn_chi(i, engine):
-            words = chi_raw[i][:].bitcast(F32)
             chi_in[i] = staged("chi_in", [128, N], BF16, 3)
-            turn(lambda g, u: words[:, 256 * g + u : 256 * (g + 1) : 2], chi_in[i], engine, by_group)
+            turn(words_of(("chi", i), chi_raw[i]), chi_in[i], engine, by_group)
 
         def turn_probe(i, engine):
-            words = probe_raw[i][:].bitcast(F32)
             probe_in[i] = staged("probe_in", [128, 2 * R], BF16, 3)
-            turn(lambda a, u: words[:, 256 * a + u : 256 * (a + 1) : 2], probe_in[i], engine, by_row_pair)
+            turn(words_of(("probe", i), probe_raw[i]), probe_in[i], engine, by_row_pair)
 
         def turn_charge(i, engine):
             words = charge[i][:].bitcast(F32)
@@ -162,7 +185,7 @@ def tile_projected_response_charge_potentials_s11_kernel(tc, chi, h_words, h_sca
                     out=acc[:],
                     lhsT=codes[:, 128 * g : 128 * (g + 1)].bitcast(FP8X4),
                     lhsT_scale=scales[:, 128 * g : 128 * (g + 1)],
-                    rhs=h_codes[:, 2 * c0 : 2 * (c0 + 512)].bitcast(FP4X4),
+                    rhs=h_codes[h][:, 1024 * g : 1024 * (g + 1)].bitcast(FP4X4),
                     rhs_scale=h_plane[:, c0 : c0 + 512],
                     start=(g == 0),
                     stop=(g == 1),
@@ -235,7 +258,7 @@ def tile_projected_response_charge_potentials_s11_kernel(tc, chi, h_words, h_sca
             nc.sync.dma_start(out=out[128 * i : 128 * (i + 1), 512 * c : 512 * (c + 1)], in_=result[:])
 
         steps = dict(
-            sc=spread_screen, w=warm_up, tc=turn_chi, tp=turn_probe, tq=turn_charge, qc=quant_chi, qp=quant_probe, qq=quant_charge,
+            xc=split_chi, xp=split_probe, sc=spread_screen, w=warm_up, tc=turn_chi, tp=turn_probe, tq=turn_charge, qc=quant_chi, qp=quant_probe, qq=quant_charge,
             la=lay_atom, qa=quant_atom, a=response, m=take_mean, c=make_charge, k=coulomb, qk=quant_kern, o=potential,
         )
         for kind, index, engine in ORDER:

from contextlib import ExitStack

import concourse.mybir as mybir
from concourse.masks import make_identity

B, N, P, R = 1024, 1024, 2048, 512
FLOPS = 2 * (B * N * N + P * R * N + B * N * P)

F32 = mybir.dt.float32
BF16 = mybir.dt.bfloat16
U32 = mybir.dt.uint32
I32 = mybir.dt.int32
U8 = mybir.dt.uint8
FP8X4 = mybir.dt.float8_e4m3fn_x4
FP4X4 = mybir.dt.float4_e2m1fn_x4
ALU = mybir.AluOpType
ACT = mybir.ActivationFunctionType

ORDER = [("w", 4, "S"), ("tc", 0, "S"), ("la", 0, "V"), ("la", 1, "V"), ("tc", 1, "S"), ("sc", 0, "S"), ("sc", 1, "S"), ("qc", 0, "S"), ("qa", 0, "S"), ("a", 0, "S"), ("qc", 1, "S"), ("a", 1, "S"), ("tp", 0, "S"), ("la", 2, "V"), ("la", 3, "V"), ("qp", 0, "S"), ("qa", 1, "S"), ("m", 0, "S"), ("tc", 2, "S"), ("tp", 1, "S"), ("a", 2, "S"), ("c", 0, "S"), ("a", 3, "S"), ("qc", 2, "S"), ("qp", 1, "S"), ("k", 0, "S"), ("k", 1, "V"), ("m", 1, "S"), ("k", 2, "S"), ("k", 3, "V"), ("tq", 0, "S"), ("tc", 3, "S"), ("tp", 2, "S"), ("a", 4, "S"), ("c", 1, "S"), ("a", 5, "S"), ("qq", 0, "S"), ("qc", 3, "S"), ("qp", 2, "S"), ("xc", 4, "V"), ("xp", 3, "V"), ("k", 4, "S"), ("k", 5, "S"), ("m", 2, "S"), ("k", 6, "V"), ("k", 7, "S"), ("tq", 1, "S"), ("tc", 4, "S"), ("tp", 3, "S"), ("qk", 0, "S"), ("qk", 1, "S"), ("a", 6, "S"), ("c", 2, "S"), ("a", 7, "S"), ("qq", 1, "S"), ("qc", 4, "S"), ("qp", 3, "S"), ("xc", 5, "V"), ("xp", 4, "V"), ("k", 8, "V"), ("o", 0, "S"), ("m", 3, "S"), ("k", 9, "S"), ("k", 10, "V"), ("k", 11, "S"), ("tq", 2, "S"), ("tc", 5, "S"), ("tp", 4, "S"), ("a", 8, "S"), ("c", 3, "S"), ("a", 9, "S"), ("qq", 2, "S"), ("qc", 5, "S"), ("qp", 4, "S"), ("xc", 6, "V"), ("xp", 5, "V"), ("k", 12, "V"), ("o", 4, "S"), ("m", 4, "S"), ("k", 13, "S"), ("k", 14, "V"), ("o", 8, "S"), ("k", 15, "V"), ("tq", 3, "S"), ("tc", 6, "S"), ("tp", 5, "S"), ("qk", 2, "S"), ("qk", 3, "S"), ("a", 10, "S"), ("c", 4, "S"), ("a", 11, "S"), ("qq", 3, "S"), ("qc", 6, "S"), ("qp", 5, "S"), ("xc", 7, "V"), ("xp", 6, "V"), ("k", 16, "S"), ("o", 1, "S"), ("m", 5, "S"), ("k", 17, "V"), ("k", 18, "S"), ("o", 5, "V"), ("k", 19, "S"), ("o", 9, "S"), ("tq", 4, "S"), ("tc", 7, "S"), ("tp", 6, "S"), ("a", 12, "S"), ("c", 5, "S"), ("a", 13, "S"), ("qq", 4, "S"), ("qc", 7, "S"), ("qp", 6, "S"), ("xp", 7, "V"), ("k", 20, "V"), ("o", 12, "S"), ("m", 6, "S"), ("k", 21, "V"), ("k", 22, "S"), ("o", 13, "S"), ("k", 23, "V"), ("o", 16, "S"), ("tq", 5, "S"), ("tp", 7, "S"), ("qk", 4, "S"), ("qk", 5, "S"), ("a", 14, "S"), ("c", 6, "S"), ("a", 15, "S"), ("qq", 5, "S"), ("qp", 7, "S"), ("k", 24, "V"), ("o", 17, "S"), ("m", 7, "S"), ("k", 25, "S"), ("o", 2, "V"), ("k", 26, "S"), ("o", 6, "V"), ("k", 27, "S"), ("o", 10, "S"), ("tq", 6, "S"), ("c", 7, "S"), ("qq", 6, "S"), ("k", 28, "V"), ("o", 14, "S"), ("k", 29, "V"), ("o", 18, "S"), ("k", 30, "S"), ("o", 20, "V"), ("k", 31, "S"), ("o", 21, "V"), ("tq", 7, "S"), ("qk", 6, "S"), ("qk", 7, "S"), ("qq", 7, "S"), ("o", 22, "S"), ("o", 24, "S"), ("o", 25, "V"), ("o", 26, "S"), ("o", 3, "V"), ("o", 7, "S"), ("o", 11, "S"), ("o", 15, "V"), ("o", 19, "S"), ("o", 23, "V"), ("o", 27, "S"), ("o", 28, "S"), ("o", 29, "V"), ("o", 30, "S"), ("o", 31, "V")]
LOADS = [("chi", 0), ("atom", 0), ("s", 0), ("hs", 0), ("hs", 1), ("hs", 2), ("hs", 3), ("chi", 1), ("h", 0), ("h", 1), ("probe", 0), ("atom", 1), ("chi", 2), ("probe", 1), ("probe", 2), ("chi", 3), ("probe", 3), ("chi", 4), ("probe", 4), ("chi", 5), ("probe", 5), ("chi", 6), ("probe", 6), ("chi", 7), ("probe", 7)]


def tile_projected_response_charge_potentials_s11_kernel(tc, chi, h_words, h_scales, screen, probe, atom, out):
    nc = tc.nc
    with ExitStack() as ctx:
        keep = ctx.enter_context(tc.tile_pool(name="keep", bufs=1))
        stage = ctx.enter_context(tc.tile_pool(name="stage", bufs=3))
        psum = ctx.enter_context(tc.psum_pool(name="psum", bufs=8))
        ctx.enter_context(tc.manual_schedule())

        def kept(name, shape, dtype):
            return keep.tile(shape, dtype, name=name, align_bytes=64)

        def staged(name, shape, dtype, bufs):
            return stage.tile(shape, dtype, name=name, bufs=bufs, align_bytes=64)

        def bank():
            return psum.tile([128, 512], F32, name="bank")

        def copy_on(engine, dst, src):
            if engine == "S":
                nc.scalar.copy(out=dst, in_=src)
            else:
                nc.vector.tensor_copy(out=dst, in_=src)

        def quantise(name, src):
            width = src.shape[1] // 4
            codes = kept(name + "_codes", [128, width], U32)
            scales = kept(name + "_scales", [128, width], U8)
            nc.vector.quantize_mx(out=codes[:].bitcast(FP8X4), scales=scales[:], in_=src)
            return codes, scales

        ident = kept("ident", [128, 128], F32)
        make_identity(nc, ident[:])
        ones = kept("ones", [128, 512], BF16)
        nc.vector.memset(ones[:], 1.0)
        screen_row = kept("screen_row", [128, N], BF16)
        nc.vector.memset(screen_row[:].bitcast(I32), 0)
        h_plane = kept("h_plane", [128, 2 * N], U8)
        nc.vector.memset(h_plane[:].bitcast(I32), 0)
        warm = kept("warm", [128, 1], F32)
        nc.scalar.activation(out=warm[:], in_=ones[:, 0:1], func=ACT.Copy)

        chi_raw, probe_raw, atom_raw = {}, {}, {}
        h_codes = {}
        for kind, i in LOADS:
            if kind == "chi":
                chi_raw[i] = kept("chi_raw%d" % i, [128, N], BF16)
                nc.sync.dma_start(out=chi_raw[i][:], in_=chi[128 * i : 128 * (i + 1), :])
            elif kind == "probe":
                probe_raw[i] = kept("probe_raw%d" % i, [128, 2 * R], BF16)
                nc.sync.dma_start(out=probe_raw[i][:], in_=probe[256 * i : 256 * (i + 1), :].rearrange("(p a) k -> p (a k)", a=2))
            elif kind == "atom":
                atom_raw[i] = kept("atom_raw%d" % i, [128, 4, 512], BF16)
                nc.sync.dma_start(out=atom_raw[i][:], in_=atom[:, 512 * i : 512 * (i + 1)].rearrange("(p j) n -> p j n", j=4))
            elif kind == "h":
                h_codes[i] = kept("h_codes%d" % i, [128, 2 * N], U8)
                nc.sync.dma_start(
                    out=h_codes[i][:].bitcast(I32).rearrange("p (g n) -> p g n", g=2),
                    in_=h_words.bitcast(I32)[:, :, 256 * i : 256 * (i + 1)].rearrange("g p n -> p g n"),
                )
            elif kind == "hs":
                nc.sync.dma_start(
                    out=h_plane[i:128:32, :].bitcast(I32).rearrange("p (g n) -> p g n", g=2),
                    in_=h_scales.bitcast(I32).rearrange("g (q r) n -> r q g n", r=4)[i],
                )
            else:
                nc.sync.dma_start(out=screen_row[0:1, :], in_=screen.rearrange("(o n) -> o n", o=1))

        def sorted_view(ap):
            return ap.rearrange("p (w e r) -> p w r e", e=2, r=8)

        def dense_view(ap):
            return ap.rearrange("p (w r e) -> p w r e", r=8, e=2)

        screen_all = kept("screen_all", [128, N], F32)
        chi_in, chi_q, neg_a, sums, mean, charge, charge_in, charge_q = {}, {}, {}, {}, {}, {}, {}, {}
        probe_in, probe_q, atom_in, atom_q, kern_in, kern_q = {}, {}, {}, {}, {}, {}

        def spread_screen(g, engine):
            acc = bank()
            nc.tensor.matmul(out=acc[:], lhsT=ones[:, 0:128], rhs=screen_row[:, 512 * g : 512 * (g + 1)], start=True, stop=True)
            copy_on(engine, dense_view(screen_all[:, 512 * g : 512 * (g + 1)]), sorted_view(acc[:]))

        def warm_up(n, engine):
            acc = bank()
            for w in range(n):
                nc.tensor.matmul(out=acc[:], lhsT=ones[:, 0:128], rhs=ones[:], start=True, stop=True)

        def turn(words_of, dst, engine, pattern):
            acc = bank()
            for c in range(4):
                nc.tensor.transpose(acc[:, 128 * c : 128 * (c + 1)], words_of(c // 2, c % 2), ident[:])
            copy_on(engine, dst[:].bitcast(F32).rearrange(pattern[0], **pattern[2]), acc[:].rearrange(pattern[1], **pattern[2]))

        by_group = ("p (g b u) -> p g b u", "p (g u b) -> p g b u", dict(g=2, u=2))
        by_row_pair = ("p (m a u) -> p m a u", "p (a u m) -> p m a u", dict(a=2, u=2))

        split = {}

        def split_words(name, raw, engine):
            split[name] = staged("split", [128, 512], F32, 4)
            copy_on(
                engine,
                split[name][:].rearrange("p (u c i) -> p c u i", u=2, i=4),
                raw[:].bitcast(F32).rearrange("p (c i u) -> p c u i", u=2, i=4),
            )

        def split_chi(i, engine):
            split_words(("chi", i), chi_raw[i], engine)

        def split_probe(i, engine):
            split_words(("probe", i), probe_raw[i], engine)

        def words_of(name, raw):
            if name in split:
                return lambda g, u: split[name][:, 256 * u + 128 * g : 256 * u + 128 * (g + 1)]
            return lambda g, u: raw[:].bitcast(F32)[:, 256 * g + u : 256 * (g + 1) : 2]

        def turn_chi(i, engine):
            chi_in[i] = staged("chi_in", [128, N], BF16, 3)
            turn(words_of(("chi", i), chi_raw[i]), chi_in[i], engine, by_group)

        def turn_probe(i, engine):
            probe_in[i] = staged("probe_in", [128, 2 * R], BF16, 3)
            turn(words_of(("probe", i), probe_raw[i]), probe_in[i], engine, by_row_pair)

        def turn_charge(i, engine):
            words = charge[i][:].bitcast(F32)
            charge_in[i] = staged("charge_in", [128, N], BF16, 3)
            turn(lambda g, u: words[:, 256 * u + 128 * g : 256 * u + 128 * (g + 1)], charge_in[i], engine, by_group)

        def quant_chi(i, engine):
            chi_q[i] = quantise("chi%d" % i, chi_in[i][:])

        def quant_probe(i, engine):
            probe_q[i] = quantise("probe%d" % i, probe_in[i][:])

        def quant_charge(i, engine):
            charge_q[i] = quantise("charge%d" % i, charge_in[i][:])

        def lay_atom(gu, engine):
            g, u = divmod(gu, 2)
            if g not in atom_in:
                atom_in[g] = kept("atom_in%d" % g, [128, 2048], BF16)
            copy_on(
                engine,
                atom_in[g][:].rearrange("p (t q r j) -> p t q r j", t=4, r=8, j=4)[:, 2 * u : 2 * u + 2],
                atom_raw[g][:].rearrange("p j (q t r) -> p t q r j", t=4, r=8)[:, 2 * u : 2 * u + 2],
            )

        def quant_atom(g, engine):
            atom_q[g] = quantise("atom%d" % g, atom_in[g][:])

        def response(ih, engine):
            i, h = divmod(ih, 2)
            if h == 0:
                neg_a[i] = staged("neg_a", [128, N], F32, 3)
                sums[i] = staged("sums", [128, 2], F32, 3)
            codes, scales = chi_q[i]
            acc = bank()
            for g in range(2):
                c0 = N * g + 512 * h
                nc.tensor.matmul_mx(
                    out=acc[:],
                    lhsT=codes[:, 128 * g : 128 * (g + 1)].bitcast(FP8X4),
                    lhsT_scale=scales[:, 128 * g : 128 * (g + 1)],
                    rhs=h_codes[h][:, 1024 * g : 1024 * (g + 1)].bitcast(FP4X4),
                    rhs_scale=h_plane[:, c0 : c0 + 512],
                    start=(g == 0),
                    stop=(g == 1),
                )
            dst = dense_view(neg_a[i][:, 512 * h : 512 * (h + 1)])
            if engine == "S":
                nc.scalar.activation(out=dst, in_=sorted_view(acc[:]), func=ACT.Copy, scale=-1.0, accum_out=sums[i][:, h : h + 1])
            else:
                nc.vector.tensor_scalar(out=dst, in0=sorted_view(acc[:]), scalar1=-1.0, scalar2=None, op0=ALU.mult, op1=ALU.add, accum_out=sums[i][:, h : h + 1])

        def take_mean(i, engine):
            mean[i] = staged("mean", [128, 1], F32, 3)
            nc.vector.tensor_scalar(out=mean[i][:], in0=sums[i][:, 0:1], scalar1=sums[i][:, 1:2], scalar2=1.0 / N, op0=ALU.add, op1=ALU.mult)

        def make_charge(i, engine):
            charge[i] = staged("charge", [128, N], BF16, 3)
            for u in range(2):
                nc.vector.scalar_tensor_tensor(
                    out=charge[i][:, 512 * u : 512 * (u + 1)].rearrange("p (w c) -> p w c", c=16),
                    in0=neg_a[i][:].rearrange("p (w u c) -> p u w c", u=2, c=16)[:, u],
                    scalar=mean[i][:],
                    in1=screen_all[:].rearrange("p (w u c) -> p u w c", u=2, c=16)[:, u],
                    op0=ALU.subtract,
                    op1=ALU.mult,
                )

        def coulomb(jg, engine):
            j, g = divmod(jg, 2)
            key = (j // 4, g)
            if j % 4 == 0:
                kern_in[key] = staged("kern_in", [128, 2048], BF16, 4)
            a_codes, a_scales = atom_q[g]
            p_codes, p_scales = probe_q[j // 2]
            cols = slice(128 * (j % 2), 128 * (j % 2 + 1))
            acc = bank()
            for t in range(4):
                nc.tensor.matmul_mx(
                    out=acc[:, 128 * t : 128 * (t + 1)],
                    lhsT=a_codes[:, 128 * t : 128 * (t + 1)].bitcast(FP8X4),
                    lhsT_scale=a_scales[:, 128 * t : 128 * (t + 1)],
                    rhs=p_codes[:, cols].bitcast(FP8X4),
                    rhs_scale=p_scales[:, cols],
                    start=True,
                    stop=True,
                )
            dst = kern_in[key][:, 512 * (j % 4) : 512 * (j % 4 + 1)]
            copy_on(engine, dst.rearrange("p (m t) -> p m t", t=4), acc[:].rearrange("p (t m) -> p m t", t=4))

        def quant_kern(cg, engine):
            key = divmod(cg, 2)
            kern_q[key] = quantise("kern%d" % cg, kern_in[key][:])

        def potential(ic, engine):
            i, c = divmod(ic, 4)
            codes, scales = charge_q[i]
            acc = bank()
            for g in range(2):
                k_codes, k_scales = kern_q[(c, g)]
                nc.tensor.matmul_mx(
                    out=acc[:],
                    lhsT=codes[:, 128 * g : 128 * (g + 1)].bitcast(FP8X4),
                    lhsT_scale=scales[:, 128 * g : 128 * (g + 1)],
                    rhs=k_codes[:].bitcast(FP8X4),
                    rhs_scale=k_scales[:],
                    start=(g == 0),
                    stop=(g == 1),
                )
            result = staged("result", [128, 512], F32, 10)
            copy_on(engine, result[:], acc[:])
            nc.sync.dma_start(out=out[128 * i : 128 * (i + 1), 512 * c : 512 * (c + 1)], in_=result[:])

        steps = dict(
            xc=split_chi, xp=split_probe, sc=spread_screen, w=warm_up, tc=turn_chi, tp=turn_probe, tq=turn_charge, qc=quant_chi, qp=quant_probe, qq=quant_charge,
            la=lay_atom, qa=quant_atom, a=response, m=take_mean, c=make_charge, k=coulomb, qk=quant_kern, o=potential,
        )
        for kind, index, engine in ORDER:
            steps[kind](index, engine)
